import numpy as np
import ml_dtypes


def mxq(x, axis, fmt="e4m3"):
    dtype, down = {"e4m3": (ml_dtypes.float8_e4m3fn, 7), "e5m2": (ml_dtypes.float8_e5m2, 14)}[fmt]
    v = np.moveaxis(np.asarray(x, np.float32).astype(ml_dtypes.bfloat16).astype(np.float64), axis, -1)
    blocks = v.reshape(v.shape[:-1] + (-1, 32))
    amax = np.abs(blocks).max(-1, keepdims=True)
    byte = np.maximum(np.where(amax > 0, np.frexp(amax)[1] - 1 + 127, 0) - down, 1)
    scale = np.exp2(byte - 127.0)
    codes = (blocks / scale).astype(np.float32).astype(dtype).astype(np.float64)
    return np.moveaxis((codes * scale).reshape(v.shape), -1, axis)


WIDE = False


def mx_kscale(k):
    if not WIDE:
        return np.ones(k)
    levels = np.array([10, -10, 5, -5, 0])
    if k % 512:
        return np.exp2(np.random.permutation(np.resize(levels, k // 32))).repeat(32)
    a = np.empty((k // 512, 16))
    for p in range(k // 512):
        a[p, :8] = np.random.permutation(np.resize(levels, 8))
        for g in range(8):
            far = levels[np.abs(levels - a[p, g]) >= 10]
            a[p, g + 8] = far[np.random.randint(len(far))]
    return np.exp2(a.ravel()).repeat(32)


BF16 = ml_dtypes.bfloat16


def bf(x):
    return np.asarray(x, np.float32).astype(BF16)


def f64(x):
    return np.asarray(x).astype(np.float64)


E2M1 = np.array([0.0, 0.5, 1.0, 1.5, 2.0, 3.0, 4.0, 6.0, -0.0, -0.5, -1.0, -1.5, -2.0, -3.0, -4.0, -6.0])


def pack_weight(w, fmt):
    k, n = w.shape
    w = f64(bf(w)).reshape(k // 32, 32, n)
    amax = np.abs(w).max(1)
    if fmt == "e4m3":
        byte = np.frexp(amax)[1] - 1 + 127 - 7
    else:
        mant, ex = np.frexp(amax / 6.0)
        byte = np.where(mant > 0.5, ex, ex - 1) + 127
    byte = np.clip(np.where(amax > 0, byte, 1), 1, 254)
    scaled = (w * np.exp2(127.0 - byte)[:, None, :]).reshape(k, n).astype(np.float32)
    by_word = np.ascontiguousarray(scaled.reshape(k // 512, 128, 4, n).transpose(0, 1, 3, 2))
    if fmt == "e4m3":
        words = by_word.astype(ml_dtypes.float8_e4m3fn).view(np.uint8)
    else:
        c = by_word.astype(ml_dtypes.float4_e2m1fn).view(np.uint8) & 0xF
        words = c[..., 0::2] | (c[..., 1::2] << 4)
    return np.ascontiguousarray(words), np.ascontiguousarray(byte.astype(np.uint8).reshape(k // 512, 16, n))


def unpack_weight(words, scales, fmt):
    g, p, n, _ = words.shape
    if fmt == "e4m3":
        vals = np.ascontiguousarray(words).view(ml_dtypes.float8_e4m3fn).astype(np.float64)
    else:
        nib = np.empty((g, p, n, 4), np.uint8)
        nib[..., 0::2] = words & 0xF
        nib[..., 1::2] = words >> 4
        vals = E2M1[nib]
    vals = vals * np.repeat(np.exp2(scales.astype(np.float64) - 127.0), 8, axis=1)[..., None]
    return vals.transpose(0, 1, 3, 2).reshape(g * 512, n)
def pack4(w):
    words, scales = pack_weight(w, "e2m1")
    return words.reshape(words.shape[0], 128, -1), scales


def unpack4(words, scales):
    return unpack_weight(words.reshape(words.shape[0], 128, -1, 2), scales, "e2m1")


def planes(Y):
    n, m = Y.shape
    b = f64(bf(Y)).reshape(n // 32, 32, m)
    amax = np.abs(b).max(1)
    byte = np.clip(np.where(amax > 0, np.frexp(amax)[1] - 1 + 127 - 7, 1), 1, 254)
    codes = (b * np.exp2(127.0 - byte)[:, None, :]).reshape(n, m).astype(np.float32).astype(ml_dtypes.float8_e4m3fn).view(np.uint8)
    words = codes.reshape(n // 512, 128, 4, m).transpose(0, 1, 3, 2)
    return np.ascontiguousarray(words), np.ascontiguousarray(byte.astype(np.uint8).reshape(n // 512, 16, m))


M, K, F, B = 1024, 2048, 1024, 1536

def setup_inputs():
    s = mx_kscale(K)
    t = mx_kscale(F)
    yields = np.random.randn(M, K) * s
    dirs = np.random.randn(K, F) / np.sqrt(K) / s[:, None] * t[None, :]
    thr = 0.3 * np.exp(0.2 * np.random.randn(F)) * t
    durs = 1.5 * np.random.randn(F, B) / np.sqrt(F) / t[:, None]
    held = np.exp(0.8 * np.random.randn(B))
    dirs_words, dirs_scales = pack4(dirs)
    durs_words, durs_scales = pack4(durs)
    return {"yields": bf(yields), "dirs_words": dirs_words, "dirs_scales": dirs_scales,
            "thresholds": bf(thr), "durs_words": durs_words, "durs_scales": durs_scales,
            "holdings": bf(held)}

def reference(yields, dirs_words, dirs_scales, thresholds, durs_words, durs_scales, holdings):
    V = unpack4(dirs_words, dirs_scales)
    D = unpack4(durs_words, durs_scales)
    thr = f64(thresholds)
    Z = mxq(f64(yields), 1, "e4m3") @ V
    H = Z - np.minimum(np.maximum(Z, -thr), thr)
    y = -(mxq(H, 1, "e4m3") @ D) * f64(holdings)
    Y = y.T
    words, scales = planes(Y)
    return y, words, scales

@@ -1,0 +1,342 @@
+from contextlib import ExitStack
+
+import concourse.mybir as mybir
+from concourse.masks import make_identity
+
+M, K, F, B = 1024, 2048, 1024, 1536
+FLOPS = 2 * M * K * F + 2 * M * F * B
+
+F32 = mybir.dt.float32
+BF16 = mybir.dt.bfloat16
+I32 = mybir.dt.int32
+U32 = mybir.dt.uint32
+U8 = mybir.dt.uint8
+FP8X4 = mybir.dt.float8_e4m3fn_x4
+FP4X4 = mybir.dt.float4_e2m1fn_x4
+ALU = mybir.AluOpType
+ACT = mybir.ActivationFunctionType
+
+P = 128
+G = 512
+KG, FG, BG = K // G, F // G, B // G
+CHUNKS = M // G
+TILES = M // P
+VECTOR_COLS = 320
+SORT_X = {}
+
+
+def tile_thresholded_duration_pnl_h1_kernel(
+    tc, yields, dirs_words, dirs_scales, thresholds, durs_words, durs_scales, holdings, out_0, out_1, out_2
+):
+    nc = tc.nc
+    with ExitStack() as ctx:
+        keep = ctx.enter_context(tc.tile_pool(name="keep", bufs=1))
+        work = ctx.enter_context(tc.tile_pool(name="work", bufs=3))
+        psum = ctx.enter_context(tc.psum_pool(name="psum", bufs=1))
+        ctx.enter_context(tc.manual_schedule(engines={mybir.EngineType.PE, mybir.EngineType.SP}))
+
+        free_banks = list(range(8))
+
+        def take_bank():
+            b = free_banks.pop(0)
+            return b, psum.tile([P, G], F32, name="bank%d" % b)
+
+        def kept(shape, dtype, name):
+            return keep.tile(shape, dtype, name=name, align_bytes=64)
+
+        ident = kept([P, P], F32, "ident")
+        make_identity(nc, ident[:])
+        v_scale_raw = [kept([P, KG, G], U8, "v_scale_raw%d" % fg) for fg in range(FG)]
+        d_scale = kept([P, FG, B], U8, "d_scale")
+        for plane in v_scale_raw + [d_scale]:
+            nc.vector.memset(plane[:].bitcast(I32), 0)
+
+        thr_bf = kept([P, FG, 4], BF16, "thr_bf")
+
+        x_raw = {}
+        v_raw = {}
+
+        def load_x(c, kg):
+            x_raw[c, kg] = kept([P, 4, G], BF16, "x_raw%d_%d" % (c, kg))
+            rows = yields[c * G : (c + 1) * G, kg * G : (kg + 1) * G]
+            nc.sync.dma_start(out=x_raw[c, kg][:], in_=rows.rearrange("(a p) k -> p a k", p=P))
+
+        def load_v(kg, fg):
+            v_raw[kg, fg] = kept([P, 2 * G], U8, "v_raw%d_%d" % (kg, fg))
+            words = dirs_words[kg, :, fg * 2 * G : (fg + 1) * 2 * G]
+            nc.sync.dma_start(out=v_raw[kg, fg][:].bitcast(I32), in_=words.bitcast(I32))
+
+        def load_scale_rows(plane, rows):
+            for q in range(4):
+                nc.sync.dma_start(
+                    out=plane[32 * q : 32 * q + 4, :, :].bitcast(I32),
+                    in_=rows[:, 4 * q : 4 * q + 4, :].rearrange("g r n -> r g n").bitcast(I32),
+                )
+
+        load_x(0, 0)
+        load_scale_rows(v_scale_raw[0], dirs_scales[:, :, :G])
+        load_v(0, 0)
+        for kg in range(1, KG):
+            load_x(0, kg)
+            load_v(kg, 0)
+        load_x(1, 0)
+        nc.sync.dma_start(out=thr_bf[:], in_=thresholds.rearrange("(g p t) -> p g t", p=P, t=4))
+        load_scale_rows(v_scale_raw[1], dirs_scales[:, :, G:])
+        load_v(0, 1)
+        load_v(1, 1)
+        load_x(1, 1)
+        load_v(2, 1)
+        load_v(3, 1)
+        load_x(1, 2)
+        load_x(1, 3)
+        d_words = []
+        for fg in range(FG):
+            d_words.append(kept([P, 2 * B], U8, "d_words%d" % fg))
+            nc.sync.dma_start(out=d_words[fg][:].bitcast(I32), in_=durs_words[fg].bitcast(I32))
+        load_scale_rows(d_scale, durs_scales)
+        hold = kept([P, B], BF16, "hold")
+        nc.sync.dma_start(out=hold[:], in_=holdings.partition_broadcast(P))
+
+        thr = kept([P, FG * 4], F32, "thr")
+        neg_thr = kept([P, FG * 4], F32, "neg_thr")
+        nc.scalar.activation(out=thr[:], in_=thr_bf[:].rearrange("p g t -> p (g t)"), func=ACT.Relu)
+        nc.scalar.activation(out=neg_thr[:], in_=thr[:], func=ACT.Copy, scale=-1.0)
+
+        v_codes, v_scales = {}, {}
+
+        def sort_v(kg, fg):
+            v_codes[kg, fg] = kept([P, 2 * G], U8, "v_codes%d_%d" % (kg, fg))
+            v_scales[kg, fg] = kept([P, G], U8, "v_scales%d_%d" % (kg, fg))
+            nc.vector.tensor_copy(
+                out=v_scales[kg, fg][:].rearrange("p (t c i) -> p c t i", t=4, i=16),
+                in_=v_scale_raw[fg][:, kg, :].rearrange("p (c i t) -> p c t i", t=4, i=16),
+            )
+            nc.vector.tensor_copy(
+                out=v_codes[kg, fg][:].rearrange("p (t c i b) -> p c t i b", t=4, i=8, b=2),
+                in_=v_raw[kg, fg][:].rearrange("p (c i t b) -> p c t i b", t=4, i=8, b=2),
+            )
+
+        def copy_turned(bank, n, dst):
+            nc.scalar.copy(
+                out=dst.bitcast(F32).rearrange("p (a r u) -> p a r u", a=n, u=2),
+                in_=bank[:, : n * 2 * P].rearrange("p (a u r) -> p a r u", a=n, u=2),
+            )
+
+        x_turned, x_codes, x_scales = {}, {}, {}
+
+        def turn_x(c, kg):
+            words = x_raw[c, kg][:].bitcast(F32)
+            presort = SORT_X.get((c, kg))
+            if presort:
+                x_sorted = work.tile([P, 4, 2, P], F32, name="x_sorted", bufs=2)
+                copy = nc.vector.tensor_copy if presort == "V" else nc.scalar.copy
+                copy(out=x_sorted[:], in_=words.rearrange("p a (w u) -> p a u w", u=2))
+            x_turned[c, kg] = work.tile([P, 4 * G], BF16, name="x_turned", align_bytes=64)
+            for half in range(2):
+                b, bank = take_bank()
+                for a in range(2):
+                    for u in range(2):
+                        j = 2 * a + u
+                        src = x_sorted[:, 2 * half + a, u, :] if presort else words[:, 2 * half + a, u : 2 * P : 2]
+                        nc.tensor.transpose(bank[:, j * P : (j + 1) * P], src, ident[:])
+                copy_turned(bank, 2, x_turned[c, kg][:, half * 2 * G : (half + 1) * 2 * G])
+                free_banks.append(b)
+
+        def quantize_x(c, kg):
+            x_codes[c, kg] = kept([P, G], U32, "x_codes%d_%d" % (c, kg))
+            x_scales[c, kg] = kept([P, G], U8, "x_scales%d_%d" % (c, kg))
+            nc.vector.quantize_mx(out=x_codes[c, kg][:].bitcast(FP8X4), scales=x_scales[c, kg][:], in_=x_turned[c, kg][:])
+
+        def z_pass(bank, c, fg, t, kg):
+            nc.tensor.matmul_mx(
+                out=bank[:],
+                lhsT=v_codes[kg, fg][:, t * 2 * P : (t + 1) * 2 * P].bitcast(FP4X4),
+                lhsT_scale=v_scales[kg, fg][:, t * P : (t + 1) * P],
+                rhs=x_codes[c, kg][:].bitcast(FP8X4),
+                rhs_scale=x_scales[c, kg][:],
+                start=(kg == 0),
+                stop=(kg == KG - 1),
+            )
+
+        h_slots, h_words, h_codes, h_scales = {}, {}, {}, {}
+
+        def shrink(b, bank, c, fg, t):
+            if t == 0:
+                h_slots[c, fg] = work.tile([P, 4, G], BF16, name="h_slots", bufs=2, align_bytes=64)
+            j = 4 * fg + t
+            above = work.tile([P, G], F32, name="above")
+            nc.scalar.activation(out=above[:], in_=bank[:], func=ACT.Relu, bias=neg_thr[:, j : j + 1], scale=1.0)
+            nc.vector.scalar_tensor_tensor(
+                out=h_slots[c, fg][:, t, :], in0=bank[:], scalar=thr[:, j : j + 1], in1=above[:], op0=ALU.add, op1=ALU.min
+            )
+            free_banks.append(b)
+
+        def z_slot(c, fg, t):
+            b, bank = take_bank()
+            for kg in range(KG):
+                z_pass(bank, c, fg, t, kg)
+            shrink(b, bank, c, fg, t)
+
+        def interleave_h(c, fg):
+            h_words[c, fg] = work.tile([P, G, 4], BF16, name="h_words", bufs=2, align_bytes=64)
+            for copy, cols in ((nc.vector.tensor_copy, slice(0, VECTOR_COLS)), (nc.scalar.copy, slice(VECTOR_COLS, G))):
+                copy(
+                    out=h_words[c, fg][:, cols, :].rearrange("p (c i) t -> p c t i", i=4),
+                    in_=h_slots[c, fg][:, :, cols].rearrange("p t (c i) -> p c t i", i=4),
+                )
+
+        def quantize_h(c, fg):
+            h_codes[c, fg] = kept([P, G], U32, "h_codes%d_%d" % (c, fg))
+            h_scales[c, fg] = kept([P, G], U8, "h_scales%d_%d" % (c, fg))
+            nc.vector.quantize_mx(
+                out=h_codes[c, fg][:].bitcast(FP8X4),
+                scales=h_scales[c, fg][:],
+                in_=h_words[c, fg][:].rearrange("p m t -> p (m t)"),
+            )
+
+        y_rows, y_pairs, y_turned, y_codes = {}, {}, {}, {}
+        y_scales = [kept([P, BG, G], U8, "y_scales%d" % c) for c in range(CHUNKS)]
+
+        def y_unit(mt, g):
+            c, cols = mt // 4, slice((mt % 4) * P, (mt % 4 + 1) * P)
+            b, bank = take_bank()
+            for fg in range(FG):
+                nc.tensor.matmul_mx(
+                    out=bank[:],
+                    lhsT=h_codes[c, fg][:, cols].bitcast(FP8X4),
+                    lhsT_scale=h_scales[c, fg][:, cols],
+                    rhs=d_words[fg][:, g * 2 * G : (g + 1) * 2 * G].bitcast(FP4X4),
+                    rhs_scale=d_scale[:, fg, g * G : (g + 1) * G],
+                    start=(fg == 0),
+                    stop=(fg == FG - 1),
+                )
+            if g == 0:
+                y_rows[mt] = work.tile([P, B], F32, name="y_rows", bufs=4)
+            bonds = slice(g * G, (g + 1) * G)
+            nc.vector.scalar_tensor_tensor(
+                out=y_rows[mt][:, bonds], in0=bank[:], scalar=-1.0, in1=hold[:, bonds], op0=ALU.mult, op1=ALU.mult
+            )
+            free_banks.append(b)
+            y_pairs[mt, g] = work.tile([P, G], BF16, name="y_pairs", bufs=12, align_bytes=64)
+            (nc.vector.tensor_copy if (mt >= 6 and g == 2) else nc.scalar.copy)(
+                out=y_pairs[mt, g][:].rearrange("m (u p e) -> m u p e", u=2, e=2),
+                in_=y_rows[mt][:, bonds].rearrange("m (p u e) -> m u p e", u=2, e=2),
+            )
+            if mt == TILES - 1:
+                nc.sync.dma_start(out=out_0[mt * P : (mt + 1) * P, bonds], in_=y_rows[mt][:, bonds])
+            elif g == BG - 1:
+                nc.sync.dma_start(out=out_0[mt * P : (mt + 1) * P, :], in_=y_rows[mt][:])
+
+        def y_tile(mt):
+            for g in range(BG):
+                y_unit(mt, g)
+
+        def turn_y(units):
+            b, bank = take_bank()
+            for a, unit in enumerate(units):
+                words = y_pairs[unit][:].bitcast(F32)
+                for u in range(2):
+                    j = 2 * a + u
+                    nc.tensor.transpose(bank[:, j * P : (j + 1) * P], words[:, u * P : (u + 1) * P], ident[:])
+            turned = work.tile([P, 2 * G], BF16, name="y_turned", bufs=4, align_bytes=64)
+            copy_turned(bank, len(units), turned[:, : len(units) * G])
+            free_banks.append(b)
+            for a, unit in enumerate(units):
+                y_turned[unit] = turned[:, a * G : (a + 1) * G]
+
+        def quantize_y(mt, g):
+            if g == 0:
+                y_codes[mt] = kept([P, BG, P], U32, "y_codes%d" % mt)
+            cols = slice((mt % 4) * P, (mt % 4 + 1) * P)
+            nc.vector.quantize_mx(
+                out=y_codes[mt][:, g, :].bitcast(FP8X4), scales=y_scales[mt // 4][:, g, cols], in_=y_turned[mt, g]
+            )
+            if g == BG - 1:
+                nc.sync.dma_start(
+                    out=out_1[:, :, mt * P : (mt + 1) * P, :].rearrange("g p m t -> p g (m t)").bitcast(I32),
+                    in_=y_codes[mt][:].bitcast(I32),
+                )
+                if mt % 4 == 3:
+                    c = mt // 4
+                    for q in range(4):
+                        queue = nc.scalar if (q % 2 == 1 and c == CHUNKS - 1) else nc.sync
+                        queue.dma_start(
+                            out=out_2[:, 4 * q : 4 * q + 4, c * G : (c + 1) * G].rearrange("g r m -> r g m").bitcast(I32),
+                            in_=y_scales[c][32 * q : 32 * q + 4, :, :].bitcast(I32),
+                        )
+
+        def turn_pair(mt):
+            units = [(mt + a, g) for a in range(2) for g in range(BG)]
+            for i in range(0, len(units), 2):
+                turn_y(units[i : i + 2])
+
+        def quantize_tile(mt):
+            for g in range(BG):
+                quantize_y(mt, g)
+
+        turn_x(0, 0)
+        sort_v(0, 0)
+        quantize_x(0, 0)
+        turn_x(0, 1)
+        sort_v(1, 0)
+        quantize_x(0, 1)
+        head = [take_bank() for t in range(4)]
+        for kg in range(KG):
+            for t in range(4):
+                z_pass(head[t][1], 0, 0, t, kg)
+            nxt = kg + 2
+            if kg == KG - 1:
+                for t in range(4):
+                    shrink(head[t][0], head[t][1], 0, 0, t)
+            turn_x(nxt // KG, nxt % KG)
+            sort_v(nxt % KG, nxt // KG)
+            quantize_x(nxt // KG, nxt % KG)
+        sort_v(2, 1)
+        sort_v(3, 1)
+        interleave_h(0, 0)
+        quantize_h(0, 0)
+        z_slot(0, 1, 0)
+        turn_x(1, 2)
+        quantize_x(1, 2)
+        z_slot(0, 1, 1)
+        turn_x(1, 3)
+        quantize_x(1, 3)
+        z_slot(0, 1, 2)
+        z_slot(0, 1, 3)
+        interleave_h(0, 1)
+        quantize_h(0, 1)
+        z_slot(1, 0, 0)
+        z_slot(1, 0, 1)
+        z_slot(1, 0, 2)
+        z_slot(1, 0, 3)
+        interleave_h(1, 0)
+        quantize_h(1, 0)
+        y_tile(0)
+        z_slot(1, 1, 0)
+        z_slot(1, 1, 1)
+        y_tile(1)
+        z_slot(1, 1, 2)
+        z_slot(1, 1, 3)
+        interleave_h(1, 1)
+        quantize_h(1, 1)
+        y_tile(2)
+        turn_pair(0)
+        y_tile(3)
+        quantize_tile(0)
+        quantize_tile(1)
+        y_tile(4)
+        turn_pair(2)
+        y_tile(5)
+        quantize_tile(2)
+        quantize_tile(3)
+        y_tile(6)
+        turn_pair(4)
+        y_tile(7)
+        quantize_tile(4)
+        quantize_tile(5)
+        turn_y([(6, 0), (6, 1)])
+        turn_y([(6, 2), (7, 0)])
+        quantize_tile(6)
+        turn_y([(7, 1)])
+        turn_y([(7, 2)])
+        quantize_tile(7)

@@ -22,7 +22,6 @@ KG, FG, BG = K // G, F // G, B // G
 CHUNKS = M // G
 TILES = M // P
 VECTOR_COLS = 320
-SORT_X = {}
 
 
 def tile_thresholded_duration_pnl_h1_kernel(
@@ -33,7 +32,7 @@ def tile_thresholded_duration_pnl_h1_kernel(
         keep = ctx.enter_context(tc.tile_pool(name="keep", bufs=1))
         work = ctx.enter_context(tc.tile_pool(name="work", bufs=3))
         psum = ctx.enter_context(tc.psum_pool(name="psum", bufs=1))
-        ctx.enter_context(tc.manual_schedule(engines={mybir.EngineType.PE, mybir.EngineType.SP}))
+        ctx.enter_context(tc.manual_schedule(engines={mybir.EngineType.PE}))
 
         free_banks = list(range(8))
 
@@ -53,6 +52,7 @@ def tile_thresholded_duration_pnl_h1_kernel(
 
         thr_bf = kept([P, FG, 4], BF16, "thr_bf")
 
+        nc.scalar.dma_start(out=thr_bf[:], in_=thresholds.rearrange("(g p t) -> p g t", p=P, t=4))
         x_raw = {}
         v_raw = {}
 
@@ -73,29 +73,32 @@ def tile_thresholded_duration_pnl_h1_kernel(
                     in_=rows[:, 4 * q : 4 * q + 4, :].rearrange("g r n -> r g n").bitcast(I32),
                 )
 
-        load_x(0, 0)
-        load_scale_rows(v_scale_raw[0], dirs_scales[:, :, :G])
-        load_v(0, 0)
-        for kg in range(1, KG):
-            load_x(0, kg)
-            load_v(kg, 0)
-        load_x(1, 0)
-        nc.sync.dma_start(out=thr_bf[:], in_=thresholds.rearrange("(g p t) -> p g t", p=P, t=4))
-        load_scale_rows(v_scale_raw[1], dirs_scales[:, :, G:])
-        load_v(0, 1)
-        load_v(1, 1)
-        load_x(1, 1)
-        load_v(2, 1)
-        load_v(3, 1)
-        load_x(1, 2)
-        load_x(1, 3)
-        d_words = []
-        for fg in range(FG):
-            d_words.append(kept([P, 2 * B], U8, "d_words%d" % fg))
-            nc.sync.dma_start(out=d_words[fg][:].bitcast(I32), in_=durs_words[fg].bitcast(I32))
-        load_scale_rows(d_scale, durs_scales)
-        hold = kept([P, B], BF16, "hold")
-        nc.sync.dma_start(out=hold[:], in_=holdings.partition_broadcast(P))
+        with tc.manual_schedule(engines={mybir.EngineType.SP}):
+            load_x(0, 0)
+            load_scale_rows(v_scale_raw[0], dirs_scales[:, :, :G])
+            load_v(0, 0)
+            load_x(0, 1)
+            load_v(1, 0)
+            load_x(0, 2)
+            load_v(2, 0)
+            load_scale_rows(v_scale_raw[1], dirs_scales[:, :, G:])
+            load_v(0, 1)
+            load_x(0, 3)
+            load_v(3, 0)
+            load_v(1, 1)
+            load_x(1, 0)
+            load_v(2, 1)
+            load_v(3, 1)
+            load_x(1, 1)
+            load_x(1, 2)
+            load_x(1, 3)
+            d_words = []
+            for fg in range(FG):
+                d_words.append(kept([P, 2 * B], U8, "d_words%d" % fg))
+                nc.sync.dma_start(out=d_words[fg][:].bitcast(I32), in_=durs_words[fg].bitcast(I32))
+            load_scale_rows(d_scale, durs_scales)
+            hold = kept([P, B], BF16, "hold")
+            nc.sync.dma_start(out=hold[:], in_=holdings.partition_broadcast(P))
 
         thr = kept([P, FG * 4], F32, "thr")
         neg_thr = kept([P, FG * 4], F32, "neg_thr")
@@ -116,30 +119,33 @@ def tile_thresholded_duration_pnl_h1_kernel(
                 in_=v_raw[kg, fg][:].rearrange("p (c i t b) -> p c t i b", t=4, i=8, b=2),
             )
 
-        def copy_turned(bank, n, dst):
-            nc.scalar.copy(
+        def copy_turned(copy, bank, n, dst):
+            copy(
                 out=dst.bitcast(F32).rearrange("p (a r u) -> p a r u", a=n, u=2),
                 in_=bank[:, : n * 2 * P].rearrange("p (a u r) -> p a r u", a=n, u=2),
             )
 
-        x_turned, x_codes, x_scales = {}, {}, {}
+        x_turned, x_codes, x_scales, x_sorted = {}, {}, {}, {}
+
+        def sort_x(c, kg):
+            x_sorted[c, kg] = work.tile([P, 4, 2, P], F32, name="x_sorted", bufs=2)
+            words = x_raw[c, kg][:].bitcast(F32)
+            nc.scalar.copy(out=x_sorted[c, kg][:], in_=words.rearrange("p a (w u) -> p a u w", u=2))
 
         def turn_x(c, kg):
             words = x_raw[c, kg][:].bitcast(F32)
-            presort = SORT_X.get((c, kg))
-            if presort:
-                x_sorted = work.tile([P, 4, 2, P], F32, name="x_sorted", bufs=2)
-                copy = nc.vector.tensor_copy if presort == "V" else nc.scalar.copy
-                copy(out=x_sorted[:], in_=words.rearrange("p a (w u) -> p a u w", u=2))
             x_turned[c, kg] = work.tile([P, 4 * G], BF16, name="x_turned", align_bytes=64)
             for half in range(2):
                 b, bank = take_bank()
                 for a in range(2):
                     for u in range(2):
                         j = 2 * a + u
-                        src = x_sorted[:, 2 * half + a, u, :] if presort else words[:, 2 * half + a, u : 2 * P : 2]
+                        if (c, kg) in x_sorted:
+                            src = x_sorted[c, kg][:, 2 * half + a, u, :]
+                        else:
+                            src = words[:, 2 * half + a, u : 2 * P : 2]
                         nc.tensor.transpose(bank[:, j * P : (j + 1) * P], src, ident[:])
-                copy_turned(bank, 2, x_turned[c, kg][:, half * 2 * G : (half + 1) * 2 * G])
+                copy_turned(nc.scalar.copy, bank, 2, x_turned[c, kg][:, half * 2 * G : (half + 1) * 2 * G])
                 free_banks.append(b)
 
         def quantize_x(c, kg):
@@ -147,9 +153,13 @@ def tile_thresholded_duration_pnl_h1_kernel(
             x_scales[c, kg] = kept([P, G], U8, "x_scales%d_%d" % (c, kg))
             nc.vector.quantize_mx(out=x_codes[c, kg][:].bitcast(FP8X4), scales=x_scales[c, kg][:], in_=x_turned[c, kg][:])
 
-        def z_pass(bank, c, fg, t, kg):
+        z_banks, aboves = {}, {}
+
+        def z_pass(c, fg, t, kg):
+            if kg == 0:
+                z_banks[c, fg, t] = take_bank()
             nc.tensor.matmul_mx(
-                out=bank[:],
+                out=z_banks[c, fg, t][1][:],
                 lhsT=v_codes[kg, fg][:, t * 2 * P : (t + 1) * 2 * P].bitcast(FP4X4),
                 lhsT_scale=v_scales[kg, fg][:, t * P : (t + 1) * P],
                 rhs=x_codes[c, kg][:].bitcast(FP8X4),
@@ -160,49 +170,59 @@ def tile_thresholded_duration_pnl_h1_kernel(
 
         h_slots, h_words, h_codes, h_scales = {}, {}, {}, {}
 
-        def shrink(b, bank, c, fg, t):
+        def excess(c, fg, t):
+            j = 4 * fg + t
+            aboves[c, fg, t] = work.tile([P, G], F32, name="above", bufs=4)
+            nc.scalar.activation(
+                out=aboves[c, fg, t][:], in_=z_banks[c, fg, t][1][:], func=ACT.Relu, bias=neg_thr[:, j : j + 1], scale=1.0
+            )
+
+        def shrink(c, fg, t):
             if t == 0:
                 h_slots[c, fg] = work.tile([P, 4, G], BF16, name="h_slots", bufs=2, align_bytes=64)
             j = 4 * fg + t
-            above = work.tile([P, G], F32, name="above")
-            nc.scalar.activation(out=above[:], in_=bank[:], func=ACT.Relu, bias=neg_thr[:, j : j + 1], scale=1.0)
+            b, bank = z_banks[c, fg, t]
             nc.vector.scalar_tensor_tensor(
-                out=h_slots[c, fg][:, t, :], in0=bank[:], scalar=thr[:, j : j + 1], in1=above[:], op0=ALU.add, op1=ALU.min
+                out=h_slots[c, fg][:, t, :],
+                in0=bank[:],
+                scalar=thr[:, j : j + 1],
+                in1=aboves[c, fg, t][:],
+                op0=ALU.add,
+                op1=ALU.min,
             )
             free_banks.append(b)
 
         def z_slot(c, fg, t):
-            b, bank = take_bank()
             for kg in range(KG):
-                z_pass(bank, c, fg, t, kg)
-            shrink(b, bank, c, fg, t)
+                z_pass(c, fg, t, kg)
+            excess(c, fg, t)
 
-        def interleave_h(c, fg):
-            h_words[c, fg] = work.tile([P, G, 4], BF16, name="h_words", bufs=2, align_bytes=64)
-            for copy, cols in ((nc.vector.tensor_copy, slice(0, VECTOR_COLS)), (nc.scalar.copy, slice(VECTOR_COLS, G))):
-                copy(
-                    out=h_words[c, fg][:, cols, :].rearrange("p (c i) t -> p c t i", i=4),
-                    in_=h_slots[c, fg][:, :, cols].rearrange("p t (c i) -> p c t i", i=4),
-                )
-
-        def quantize_h(c, fg):
-            h_codes[c, fg] = kept([P, G], U32, "h_codes%d_%d" % (c, fg))
-            h_scales[c, fg] = kept([P, G], U8, "h_scales%d_%d" % (c, fg))
-            nc.vector.quantize_mx(
-                out=h_codes[c, fg][:].bitcast(FP8X4),
-                scales=h_scales[c, fg][:],
-                in_=h_words[c, fg][:].rearrange("p m t -> p (m t)"),
+        def interleave_h(copy, c, fg, lo, hi):
+            if (c, fg) not in h_words:
+                h_words[c, fg] = work.tile([P, G, 4], BF16, name="h_words", bufs=2, align_bytes=64)
+                h_codes[c, fg] = kept([P, G], U32, "h_codes%d_%d" % (c, fg))
+                h_scales[c, fg] = kept([P, G], U8, "h_scales%d_%d" % (c, fg))
+            copy(
+                out=h_words[c, fg][:, lo:hi, :].rearrange("p (c i) t -> p c t i", i=4),
+                in_=h_slots[c, fg][:, :, lo:hi].rearrange("p t (c i) -> p c t i", i=4),
             )
 
-        y_rows, y_pairs, y_turned, y_codes = {}, {}, {}, {}
+        def quantize_h(c, fg, lo, hi):
+            nc.vector.quantize_mx(
+                out=h_codes[c, fg][:, lo:hi].bitcast(FP8X4),
+                scales=h_scales[c, fg][:, lo:hi],
+                in_=h_words[c, fg][:, lo:hi, :].rearrange("p m t -> p (m t)"),
+            )
+
+        y_banks, y_rows, y_pairs, y_turned, y_codes = {}, {}, {}, {}, {}
         y_scales = [kept([P, BG, G], U8, "y_scales%d" % c) for c in range(CHUNKS)]
 
-        def y_unit(mt, g):
+        def y_product(mt, g):
             c, cols = mt // 4, slice((mt % 4) * P, (mt % 4 + 1) * P)
-            b, bank = take_bank()
+            y_banks[mt, g] = take_bank()
             for fg in range(FG):
                 nc.tensor.matmul_mx(
-                    out=bank[:],
+                    out=y_banks[mt, g][1][:],
                     lhsT=h_codes[c, fg][:, cols].bitcast(FP8X4),
                     lhsT_scale=h_scales[c, fg][:, cols],
                     rhs=d_words[fg][:, g * 2 * G : (g + 1) * 2 * G].bitcast(FP4X4),
@@ -210,6 +230,9 @@ def tile_thresholded_duration_pnl_h1_kernel(
                     start=(fg == 0),
                     stop=(fg == FG - 1),
                 )
+
+        def y_finish(mt, g, round_on=None):
+            b, bank = y_banks[mt, g]
             if g == 0:
                 y_rows[mt] = work.tile([P, B], F32, name="y_rows", bufs=4)
             bonds = slice(g * G, (g + 1) * G)
@@ -217,126 +240,168 @@ def tile_thresholded_duration_pnl_h1_kernel(
                 out=y_rows[mt][:, bonds], in0=bank[:], scalar=-1.0, in1=hold[:, bonds], op0=ALU.mult, op1=ALU.mult
             )
             free_banks.append(b)
-            y_pairs[mt, g] = work.tile([P, G], BF16, name="y_pairs", bufs=12, align_bytes=64)
-            (nc.vector.tensor_copy if (mt >= 6 and g == 2) else nc.scalar.copy)(
-                out=y_pairs[mt, g][:].rearrange("m (u p e) -> m u p e", u=2, e=2),
-                in_=y_rows[mt][:, bonds].rearrange("m (p u e) -> m u p e", u=2, e=2),
-            )
             if mt == TILES - 1:
                 nc.sync.dma_start(out=out_0[mt * P : (mt + 1) * P, bonds], in_=y_rows[mt][:, bonds])
             elif g == BG - 1:
                 nc.sync.dma_start(out=out_0[mt * P : (mt + 1) * P, :], in_=y_rows[mt][:])
 
-        def y_tile(mt):
-            for g in range(BG):
-                y_unit(mt, g)
+        def y_round(copy, mt, g):
+            y_pairs[mt, g] = work.tile([P, G], BF16, name="y_pairs", bufs=12, align_bytes=64)
+            copy(
+                out=y_pairs[mt, g][:].rearrange("m (u p e) -> m u p e", u=2, e=2),
+                in_=y_rows[mt][:, g * G : (g + 1) * G].rearrange("m (p u e) -> m u p e", u=2, e=2),
+            )
 
-        def turn_y(units):
+        def turn_y(tiles, g, copy=nc.scalar.copy):
             b, bank = take_bank()
-            for a, unit in enumerate(units):
-                words = y_pairs[unit][:].bitcast(F32)
+            for a, mt in enumerate(tiles):
+                words = y_pairs[mt, g][:].bitcast(F32)
                 for u in range(2):
                     j = 2 * a + u
                     nc.tensor.transpose(bank[:, j * P : (j + 1) * P], words[:, u * P : (u + 1) * P], ident[:])
-            turned = work.tile([P, 2 * G], BF16, name="y_turned", bufs=4, align_bytes=64)
-            copy_turned(bank, len(units), turned[:, : len(units) * G])
+            turned = work.tile([P, 2 * G], BF16, name="y_turned", bufs=6, align_bytes=64)
+            y_turned[tiles, g] = turned[:, : len(tiles) * G]
+            copy_turned(copy, bank, len(tiles), y_turned[tiles, g])
             free_banks.append(b)
-            for a, unit in enumerate(units):
-                y_turned[unit] = turned[:, a * G : (a + 1) * G]
 
-        def quantize_y(mt, g):
+        def quantize_y(tiles, g):
+            n, first = len(tiles) * P, tiles[0] * P
             if g == 0:
-                y_codes[mt] = kept([P, BG, P], U32, "y_codes%d" % mt)
-            cols = slice((mt % 4) * P, (mt % 4 + 1) * P)
+                y_codes[tiles] = kept([P, BG, n], U32, "y_codes%d" % tiles[0])
+            c = first // G
             nc.vector.quantize_mx(
-                out=y_codes[mt][:, g, :].bitcast(FP8X4), scales=y_scales[mt // 4][:, g, cols], in_=y_turned[mt, g]
+                out=y_codes[tiles][:, g, :].bitcast(FP8X4),
+                scales=y_scales[c][:, g, first - c * G : first - c * G + n],
+                in_=y_turned[tiles, g],
             )
-            if g == BG - 1:
-                nc.sync.dma_start(
-                    out=out_1[:, :, mt * P : (mt + 1) * P, :].rearrange("g p m t -> p g (m t)").bitcast(I32),
-                    in_=y_codes[mt][:].bitcast(I32),
+
+        def store_codes(tiles, lo, hi):
+            n, first = len(tiles) * P, tiles[0] * P
+            nc.sync.dma_start(
+                out=out_1[lo:hi, :, first : first + n, :].rearrange("g p m t -> p g (m t)").bitcast(I32),
+                in_=y_codes[tiles][:, lo:hi, :].bitcast(I32),
+            )
+
+        def store_scales(first_tile, end_tile, queues):
+            c, lo, hi = first_tile // 4, first_tile * P, end_tile * P
+            for q in range(4):
+                queues[q % len(queues)].dma_start(
+                    out=out_2[:, 4 * q : 4 * q + 4, lo:hi].rearrange("g r m -> r g m").bitcast(I32),
+                    in_=y_scales[c][32 * q : 32 * q + 4, :, lo - c * G : hi - c * G].bitcast(I32),
                 )
-                if mt % 4 == 3:
-                    c = mt // 4
-                    for q in range(4):
-                        queue = nc.scalar if (q % 2 == 1 and c == CHUNKS - 1) else nc.sync
-                        queue.dma_start(
-                            out=out_2[:, 4 * q : 4 * q + 4, c * G : (c + 1) * G].rearrange("g r m -> r g m").bitcast(I32),
-                            in_=y_scales[c][32 * q : 32 * q + 4, :, :].bitcast(I32),
-                        )
 
-        def turn_pair(mt):
-            units = [(mt + a, g) for a in range(2) for g in range(BG)]
-            for i in range(0, len(units), 2):
-                turn_y(units[i : i + 2])
+        V, S = nc.vector.tensor_copy, nc.scalar.copy
+        half = G // 2
 
-        def quantize_tile(mt):
+        def y_unit(mt, g, copy=S):
+            y_product(mt, g)
+            y_finish(mt, g)
+            y_round(copy, mt, g)
+
+        def y_tile(mt):
             for g in range(BG):
-                quantize_y(mt, g)
+                y_unit(mt, g, V if (g == 2 and mt >= 4) else S)
 
-        turn_x(0, 0)
-        sort_v(0, 0)
-        quantize_x(0, 0)
-        turn_x(0, 1)
-        sort_v(1, 0)
-        quantize_x(0, 1)
-        head = [take_bank() for t in range(4)]
-        for kg in range(KG):
+        def turn_pair(tiles):
+            for g in range(BG):
+                turn_y(tiles, g)
+
+        def quantize_pair(tiles):
+            for g in range(BG):
+                quantize_y(tiles, g)
+            store_codes(tiles, 0, BG)
+            if tiles[-1] == 3:
+                store_scales(0, 4, [nc.sync])
+
+        def z_full(c, fg, t):
+            z_slot(c, fg, t)
+            shrink(c, fg, t)
+            if t == 3 and fg == 0:
+                interleave_h(V, c, fg, 0, 320)
+                interleave_h(S, c, fg, 320, G)
+                quantize_h(c, fg, 0, G)
+            elif t == 3:
+                interleave_h(V, c, fg, 0, half)
+                quantize_h(c, fg, 0, half)
+                interleave_h(S, c, fg, half, G)
+                quantize_h(c, fg, half, G)
+
+        def x_part(c, kg):
+            turn_x(c, kg)
+            quantize_x(c, kg)
+
+        def head_pass(kg):
             for t in range(4):
-                z_pass(head[t][1], 0, 0, t, kg)
-            nxt = kg + 2
-            if kg == KG - 1:
-                for t in range(4):
-                    shrink(head[t][0], head[t][1], 0, 0, t)
-            turn_x(nxt // KG, nxt % KG)
-            sort_v(nxt % KG, nxt // KG)
-            quantize_x(nxt // KG, nxt % KG)
-        sort_v(2, 1)
-        sort_v(3, 1)
-        interleave_h(0, 0)
-        quantize_h(0, 0)
-        z_slot(0, 1, 0)
-        turn_x(1, 2)
-        quantize_x(1, 2)
-        z_slot(0, 1, 1)
-        turn_x(1, 3)
-        quantize_x(1, 3)
-        z_slot(0, 1, 2)
-        z_slot(0, 1, 3)
-        interleave_h(0, 1)
-        quantize_h(0, 1)
-        z_slot(1, 0, 0)
-        z_slot(1, 0, 1)
-        z_slot(1, 0, 2)
-        z_slot(1, 0, 3)
-        interleave_h(1, 0)
-        quantize_h(1, 0)
+                z_pass(0, 0, t, kg)
+
+        def planes(tiles):
+            turn_pair(tiles)
+            quantize_pair(tiles)
+
+        with tc.manual_schedule():
+            turn_x(0, 0)
+            sort_v(0, 0)
+            quantize_x(0, 0)
+            turn_x(0, 1)
+            sort_v(1, 0)
+            head_pass(0)
+            quantize_x(0, 1)
+            sort_v(2, 0)
+            turn_x(0, 2)
+            sort_v(0, 1)
+            head_pass(1)
+            sort_v(3, 0)
+            quantize_x(0, 2)
+            turn_x(0, 3)
+            sort_v(1, 1)
+            head_pass(2)
+            sort_v(2, 1)
+            quantize_x(0, 3)
+            turn_x(1, 0)
+            sort_v(3, 1)
+            head_pass(3)
+            quantize_x(1, 0)
+            for t in range(4):
+                excess(0, 0, t)
+                shrink(0, 0, t)
+        interleave_h(V, 0, 0, 0, 320)
+        interleave_h(S, 0, 0, 320, G)
+        quantize_h(0, 0, 0, G)
+        x_part(1, 1)
+        z_full(0, 1, 0)
+        x_part(1, 2)
+        z_full(0, 1, 1)
+        x_part(1, 3)
+        z_full(0, 1, 2)
+        z_full(0, 1, 3)
+        z_full(1, 0, 0)
+        z_full(1, 0, 1)
+        z_full(1, 0, 2)
+        z_full(1, 0, 3)
         y_tile(0)
-        z_slot(1, 1, 0)
-        z_slot(1, 1, 1)
+        z_full(1, 1, 0)
+        z_full(1, 1, 1)
         y_tile(1)
-        z_slot(1, 1, 2)
-        z_slot(1, 1, 3)
-        interleave_h(1, 1)
-        quantize_h(1, 1)
+        z_full(1, 1, 2)
+        z_full(1, 1, 3)
         y_tile(2)
-        turn_pair(0)
+        turn_pair((0, 1,))
+        quantize_pair((0, 1,))
         y_tile(3)
-        quantize_tile(0)
-        quantize_tile(1)
         y_tile(4)
-        turn_pair(2)
+        turn_pair((2, 3,))
         y_tile(5)
-        quantize_tile(2)
-        quantize_tile(3)
+        quantize_pair((2, 3,))
         y_tile(6)
-        turn_pair(4)
-        y_tile(7)
-        quantize_tile(4)
-        quantize_tile(5)
-        turn_y([(6, 0), (6, 1)])
-        turn_y([(6, 2), (7, 0)])
-        quantize_tile(6)
-        turn_y([(7, 1)])
-        turn_y([(7, 2)])
-        quantize_tile(7)
+        turn_pair((4, 5,))
+        y_unit(7, 0, S)
+        y_unit(7, 1, S)
+        quantize_pair((4, 5,))
+        turn_pair((6,))
+        y_unit(7, 2, V)
+        quantize_pair((6,))
+        for g in range(BG):
+            turn_y((7,), g, V if g == 2 else S)
+            quantize_y((7,), g)
+        store_codes((7,), 0, 3)
+        store_scales(4, 8, [nc.sync, nc.scalar])

@@ -50,6 +50,11 @@ def tile_thresholded_duration_pnl_h1_kernel(
         for plane in v_scale_raw + [d_scale]:
             nc.vector.memset(plane[:].bitcast(I32), 0)
 
+        zeros = kept([P, 4 * G], BF16, "zeros")
+        warm_codes = kept([P, G], U32, "warm_codes")
+        warm_scales = kept([P, G], U8, "warm_scales")
+        nc.vector.memset(zeros[:].bitcast(I32), 0)
+        nc.vector.quantize_mx(out=warm_codes[:].bitcast(FP8X4), scales=warm_scales[:], in_=zeros[:])
         thr_bf = kept([P, FG, 4], BF16, "thr_bf")
 
         nc.scalar.dma_start(out=thr_bf[:], in_=thresholds.rearrange("(g p t) -> p g t", p=P, t=4))
@@ -240,7 +245,7 @@ def tile_thresholded_duration_pnl_h1_kernel(
                 out=y_rows[mt][:, bonds], in0=bank[:], scalar=-1.0, in1=hold[:, bonds], op0=ALU.mult, op1=ALU.mult
             )
             free_banks.append(b)
-            if mt == TILES - 1:
+            if True:
                 nc.sync.dma_start(out=out_0[mt * P : (mt + 1) * P, bonds], in_=y_rows[mt][:, bonds])
             elif g == BG - 1:
                 nc.sync.dma_start(out=out_0[mt * P : (mt + 1) * P, :], in_=y_rows[mt][:])
@@ -340,6 +345,18 @@ def tile_thresholded_duration_pnl_h1_kernel(
 
         with tc.manual_schedule():
             turn_x(0, 0)
+            b, bank = take_bank()
+            for i in range(2):
+                nc.tensor.matmul_mx(
+                    out=bank[:],
+                    lhsT=v_raw[0, 0][:, : 2 * P].bitcast(FP4X4),
+                    lhsT_scale=warm_scales[:, :P],
+                    rhs=warm_codes[:].bitcast(FP8X4),
+                    rhs_scale=warm_scales[:],
+                    start=True,
+                    stop=True,
+                )
+            free_banks.append(b)
             sort_v(0, 0)
             quantize_x(0, 0)
             turn_x(0, 1)
@@ -350,13 +367,13 @@ def tile_thresholded_duration_pnl_h1_kernel(
             turn_x(0, 2)
             sort_v(0, 1)
             head_pass(1)
-            sort_v(3, 0)
             quantize_x(0, 2)
+            sort_v(3, 0)
             turn_x(0, 3)
             sort_v(1, 1)
             head_pass(2)
-            sort_v(2, 1)
             quantize_x(0, 3)
+            sort_v(2, 1)
             turn_x(1, 0)
             sort_v(3, 1)
             head_pass(3)
@@ -369,8 +386,8 @@ def tile_thresholded_duration_pnl_h1_kernel(
         quantize_h(0, 0, 0, G)
         x_part(1, 1)
         z_full(0, 1, 0)
-        x_part(1, 2)
         z_full(0, 1, 1)
+        x_part(1, 2)
         x_part(1, 3)
         z_full(0, 1, 2)
         z_full(0, 1, 3)
@@ -385,20 +402,20 @@ def tile_thresholded_duration_pnl_h1_kernel(
         z_full(1, 1, 2)
         z_full(1, 1, 3)
         y_tile(2)
+        y_tile(3)
         turn_pair((0, 1,))
         quantize_pair((0, 1,))
-        y_tile(3)
         y_tile(4)
-        turn_pair((2, 3,))
         y_tile(5)
+        turn_pair((2, 3,))
         quantize_pair((2, 3,))
         y_tile(6)
         turn_pair((4, 5,))
         y_unit(7, 0, S)
         y_unit(7, 1, S)
-        quantize_pair((4, 5,))
-        turn_pair((6,))
         y_unit(7, 2, V)
+        turn_pair((6,))
+        quantize_pair((4, 5,))
         quantize_pair((6,))
         for g in range(BG):
             turn_y((7,), g, V if g == 2 else S)

@@ -45,10 +45,28 @@ def tile_thresholded_duration_pnl_h1_kernel(
 
         ident = kept([P, P], F32, "ident")
         make_identity(nc, ident[:])
-        v_scale_raw = [kept([P, KG, G], U8, "v_scale_raw%d" % fg) for fg in range(FG)]
+        v_scale_packed = kept([P, F], U8, "v_scale_packed")
+        v_planes = [kept([P, F], U8, "v_plane%d" % kg) for kg in range(KG)]
         d_scale = kept([P, FG, B], U8, "d_scale")
-        for plane in v_scale_raw + [d_scale]:
+        for plane in [v_scale_packed] + v_planes[1:] + [d_scale]:
             nc.vector.memset(plane[:].bitcast(I32), 0)
+
+        def load_v_scales():
+            for q in range(4):
+                nc.sync.dma_start(
+                    out=v_scale_packed[32 * q : 32 * q + 16, :].bitcast(I32),
+                    in_=dirs_scales[:, 4 * q : 4 * q + 4, :].bitcast(I32),
+                )
+            nc.vector.tensor_copy(
+                out=v_planes[0][:].rearrange("p (t c i) -> p c t i", t=4, i=16),
+                in_=v_scale_packed[:].rearrange("p (c i t) -> p c t i", t=4, i=16),
+            )
+
+        def lift_v_scales(kg):
+            nc.sync.dma_start(
+                out=v_planes[kg][:112, :].bitcast(I32), in_=v_planes[0][4 * kg : 4 * kg + 112, :].bitcast(I32)
+            )
+
 
         zeros = kept([P, 4 * G], BF16, "zeros")
         warm_codes = kept([P, G], U32, "warm_codes")
@@ -80,21 +98,23 @@ def tile_thresholded_duration_pnl_h1_kernel(
 
         with tc.manual_schedule(engines={mybir.EngineType.SP}):
             load_x(0, 0)
-            load_scale_rows(v_scale_raw[0], dirs_scales[:, :, :G])
+            load_v_scales()
             load_v(0, 0)
             load_x(0, 1)
             load_v(1, 0)
             load_x(0, 2)
             load_v(2, 0)
-            load_scale_rows(v_scale_raw[1], dirs_scales[:, :, G:])
-            load_v(0, 1)
+            lift_v_scales(1)
             load_x(0, 3)
             load_v(3, 0)
-            load_v(1, 1)
+            lift_v_scales(2)
+            lift_v_scales(3)
             load_x(1, 0)
+            load_v(0, 1)
+            load_x(1, 1)
+            load_v(1, 1)
             load_v(2, 1)
             load_v(3, 1)
-            load_x(1, 1)
             load_x(1, 2)
             load_x(1, 3)
             d_words = []
@@ -114,11 +134,6 @@ def tile_thresholded_duration_pnl_h1_kernel(
 
         def sort_v(kg, fg):
             v_codes[kg, fg] = kept([P, 2 * G], U8, "v_codes%d_%d" % (kg, fg))
-            v_scales[kg, fg] = kept([P, G], U8, "v_scales%d_%d" % (kg, fg))
-            nc.vector.tensor_copy(
-                out=v_scales[kg, fg][:].rearrange("p (t c i) -> p c t i", t=4, i=16),
-                in_=v_scale_raw[fg][:, kg, :].rearrange("p (c i t) -> p c t i", t=4, i=16),
-            )
             nc.vector.tensor_copy(
                 out=v_codes[kg, fg][:].rearrange("p (t c i b) -> p c t i b", t=4, i=8, b=2),
                 in_=v_raw[kg, fg][:].rearrange("p (c i t b) -> p c t i b", t=4, i=8, b=2),
@@ -135,7 +150,7 @@ def tile_thresholded_duration_pnl_h1_kernel(
         def sort_x(c, kg):
             x_sorted[c, kg] = work.tile([P, 4, 2, P], F32, name="x_sorted", bufs=2)
             words = x_raw[c, kg][:].bitcast(F32)
-            nc.scalar.copy(out=x_sorted[c, kg][:], in_=words.rearrange("p a (w u) -> p a u w", u=2))
+            nc.vector.tensor_copy(out=x_sorted[c, kg][:], in_=words.rearrange("p a (w u) -> p a u w", u=2))
 
         def turn_x(c, kg):
             words = x_raw[c, kg][:].bitcast(F32)
@@ -166,7 +181,7 @@ def tile_thresholded_duration_pnl_h1_kernel(
             nc.tensor.matmul_mx(
                 out=z_banks[c, fg, t][1][:],
                 lhsT=v_codes[kg, fg][:, t * 2 * P : (t + 1) * 2 * P].bitcast(FP4X4),
-                lhsT_scale=v_scales[kg, fg][:, t * P : (t + 1) * P],
+                lhsT_scale=v_planes[kg][:, (2 * t + fg) * P : (2 * t + fg + 1) * P],
                 rhs=x_codes[c, kg][:].bitcast(FP8X4),
                 rhs_scale=x_scales[c, kg][:],
                 start=(kg == 0),
@@ -362,19 +377,22 @@ def tile_thresholded_duration_pnl_h1_kernel(
             turn_x(0, 1)
             sort_v(1, 0)
             head_pass(0)
+            sort_x(0, 2)
             quantize_x(0, 1)
             sort_v(2, 0)
             turn_x(0, 2)
-            sort_v(0, 1)
             head_pass(1)
+            sort_x(0, 3)
             quantize_x(0, 2)
             sort_v(3, 0)
             turn_x(0, 3)
-            sort_v(1, 1)
+            sort_x(1, 0)
             head_pass(2)
             quantize_x(0, 3)
-            sort_v(2, 1)
+            sort_v(0, 1)
             turn_x(1, 0)
+            sort_v(1, 1)
+            sort_v(2, 1)
             sort_v(3, 1)
             head_pass(3)
             quantize_x(1, 0)

from contextlib import ExitStack

import concourse.mybir as mybir
from concourse.masks import make_identity

M, K, F, B = 1024, 2048, 1024, 1536
FLOPS = 2 * M * K * F + 2 * M * F * B

F32 = mybir.dt.float32
BF16 = mybir.dt.bfloat16
I32 = mybir.dt.int32
U32 = mybir.dt.uint32
U8 = mybir.dt.uint8
FP8X4 = mybir.dt.float8_e4m3fn_x4
FP4X4 = mybir.dt.float4_e2m1fn_x4
ALU = mybir.AluOpType
ACT = mybir.ActivationFunctionType

P = 128
G = 512
KG, FG, BG = K // G, F // G, B // G
CHUNKS = M // G
TILES = M // P
VECTOR_COLS = 320


def tile_thresholded_duration_pnl_h1_kernel(
    tc, yields, dirs_words, dirs_scales, thresholds, durs_words, durs_scales, holdings, out_0, out_1, out_2
):
    nc = tc.nc
    with ExitStack() as ctx:
        keep = ctx.enter_context(tc.tile_pool(name="keep", bufs=1))
        work = ctx.enter_context(tc.tile_pool(name="work", bufs=3))
        psum = ctx.enter_context(tc.psum_pool(name="psum", bufs=1))
        ctx.enter_context(tc.manual_schedule(engines={mybir.EngineType.PE}))

        free_banks = list(range(8))

        def take_bank():
            b = free_banks.pop(0)
            return b, psum.tile([P, G], F32, name="bank%d" % b)

        def kept(shape, dtype, name):
            return keep.tile(shape, dtype, name=name, align_bytes=64)

        ident = kept([P, P], F32, "ident")
        make_identity(nc, ident[:])
        v_scale_packed = kept([P, F], U8, "v_scale_packed")
        v_planes = [kept([P, F], U8, "v_plane%d" % kg) for kg in range(KG)]
        d_scale = kept([P, FG, B], U8, "d_scale")
        for plane in [v_scale_packed] + v_planes[1:] + [d_scale]:
            nc.vector.memset(plane[:].bitcast(I32), 0)

        def load_v_scales():
            for q in range(4):
                nc.sync.dma_start(
                    out=v_scale_packed[32 * q : 32 * q + 16, :].bitcast(I32),
                    in_=dirs_scales[:, 4 * q : 4 * q + 4, :].bitcast(I32),
                )
            nc.vector.tensor_copy(
                out=v_planes[0][:].rearrange("p (t c i) -> p c t i", t=4, i=16),
                in_=v_scale_packed[:].rearrange("p (c i t) -> p c t i", t=4, i=16),
            )

        def lift_v_scales(kg):
            nc.sync.dma_start(
                out=v_planes[kg][:112, :].bitcast(I32), in_=v_planes[0][4 * kg : 4 * kg + 112, :].bitcast(I32)
            )


        zeros = kept([P, 4 * G], BF16, "zeros")
        warm_codes = kept([P, G], U32, "warm_codes")
        warm_scales = kept([P, G], U8, "warm_scales")
        nc.vector.memset(zeros[:].bitcast(I32), 0)
        nc.vector.quantize_mx(out=warm_codes[:].bitcast(FP8X4), scales=warm_scales[:], in_=zeros[:])
        thr_bf = kept([P, FG, 4], BF16, "thr_bf")

        nc.scalar.dma_start(out=thr_bf[:], in_=thresholds.rearrange("(g p t) -> p g t", p=P, t=4))
        x_raw = {}
        v_raw = {}

        def load_x(c, kg):
            x_raw[c, kg] = kept([P, 4, G], BF16, "x_raw%d_%d" % (c, kg))
            rows = yields[c * G : (c + 1) * G, kg * G : (kg + 1) * G]
            nc.sync.dma_start(out=x_raw[c, kg][:], in_=rows.rearrange("(a p) k -> p a k", p=P))

        def load_v(kg, fg):
            v_raw[kg, fg] = kept([P, 2 * G], U8, "v_raw%d_%d" % (kg, fg))
            words = dirs_words[kg, :, fg * 2 * G : (fg + 1) * 2 * G]
            nc.sync.dma_start(out=v_raw[kg, fg][:].bitcast(I32), in_=words.bitcast(I32))

        def load_scale_rows(plane, rows):
            for q in range(4):
                nc.sync.dma_start(
                    out=plane[32 * q : 32 * q + 4, :, :].bitcast(I32),
                    in_=rows[:, 4 * q : 4 * q + 4, :].rearrange("g r n -> r g n").bitcast(I32),
                )

        with tc.manual_schedule(engines={mybir.EngineType.SP}):
            load_x(0, 0)
            load_v_scales()
            load_v(0, 0)
            load_x(0, 1)
            load_v(1, 0)
            load_x(0, 2)
            load_v(2, 0)
            lift_v_scales(1)
            load_x(0, 3)
            load_v(3, 0)
            lift_v_scales(2)
            lift_v_scales(3)
            load_x(1, 0)
            load_v(0, 1)
            load_x(1, 1)
            load_v(1, 1)
            load_v(2, 1)
            load_v(3, 1)
            load_x(1, 2)
            load_x(1, 3)
            d_words = []
            for fg in range(FG):
                d_words.append(kept([P, 2 * B], U8, "d_words%d" % fg))
                nc.sync.dma_start(out=d_words[fg][:].bitcast(I32), in_=durs_words[fg].bitcast(I32))
            load_scale_rows(d_scale, durs_scales)
            hold = kept([P, B], BF16, "hold")
            nc.sync.dma_start(out=hold[:], in_=holdings.partition_broadcast(P))

        thr = kept([P, FG * 4], F32, "thr")
        neg_thr = kept([P, FG * 4], F32, "neg_thr")
        nc.scalar.activation(out=thr[:], in_=thr_bf[:].rearrange("p g t -> p (g t)"), func=ACT.Relu)
        nc.scalar.activation(out=neg_thr[:], in_=thr[:], func=ACT.Copy, scale=-1.0)

        v_codes, v_scales = {}, {}

        def sort_v(kg, fg):
            v_codes[kg, fg] = kept([P, 2 * G], U8, "v_codes%d_%d" % (kg, fg))
            nc.vector.tensor_copy(
                out=v_codes[kg, fg][:].rearrange("p (t c i b) -> p c t i b", t=4, i=8, b=2),
                in_=v_raw[kg, fg][:].rearrange("p (c i t b) -> p c t i b", t=4, i=8, b=2),
            )

        def copy_turned(copy, bank, n, dst):
            copy(
                out=dst.bitcast(F32).rearrange("p (a r u) -> p a r u", a=n, u=2),
                in_=bank[:, : n * 2 * P].rearrange("p (a u r) -> p a r u", a=n, u=2),
            )

        x_turned, x_codes, x_scales, x_sorted = {}, {}, {}, {}

        def sort_x(c, kg):
            x_sorted[c, kg] = work.tile([P, 4, 2, P], F32, name="x_sorted", bufs=2)
            words = x_raw[c, kg][:].bitcast(F32)
            nc.vector.tensor_copy(out=x_sorted[c, kg][:], in_=words.rearrange("p a (w u) -> p a u w", u=2))

        def turn_x(c, kg):
            words = x_raw[c, kg][:].bitcast(F32)
            x_turned[c, kg] = work.tile([P, 4 * G], BF16, name="x_turned", align_bytes=64)
            for half in range(2):
                b, bank = take_bank()
                for a in range(2):
                    for u in range(2):
                        j = 2 * a + u
                        if (c, kg) in x_sorted:
                            src = x_sorted[c, kg][:, 2 * half + a, u, :]
                        else:
                            src = words[:, 2 * half + a, u : 2 * P : 2]
                        nc.tensor.transpose(bank[:, j * P : (j + 1) * P], src, ident[:])
                copy_turned(nc.scalar.copy, bank, 2, x_turned[c, kg][:, half * 2 * G : (half + 1) * 2 * G])
                free_banks.append(b)

        def quantize_x(c, kg):
            x_codes[c, kg] = kept([P, G], U32, "x_codes%d_%d" % (c, kg))
            x_scales[c, kg] = kept([P, G], U8, "x_scales%d_%d" % (c, kg))
            nc.vector.quantize_mx(out=x_codes[c, kg][:].bitcast(FP8X4), scales=x_scales[c, kg][:], in_=x_turned[c, kg][:])

        z_banks, aboves = {}, {}

        def z_pass(c, fg, t, kg):
            if kg == 0:
                z_banks[c, fg, t] = take_bank()
            nc.tensor.matmul_mx(
                out=z_banks[c, fg, t][1][:],
                lhsT=v_codes[kg, fg][:, t * 2 * P : (t + 1) * 2 * P].bitcast(FP4X4),
                lhsT_scale=v_planes[kg][:, (2 * t + fg) * P : (2 * t + fg + 1) * P],
                rhs=x_codes[c, kg][:].bitcast(FP8X4),
                rhs_scale=x_scales[c, kg][:],
                start=(kg == 0),
                stop=(kg == KG - 1),
            )

        h_slots, h_words, h_codes, h_scales = {}, {}, {}, {}

        def excess(c, fg, t):
            j = 4 * fg + t
            aboves[c, fg, t] = work.tile([P, G], F32, name="above", bufs=4)
            nc.scalar.activation(
                out=aboves[c, fg, t][:], in_=z_banks[c, fg, t][1][:], func=ACT.Relu, bias=neg_thr[:, j : j + 1], scale=1.0
            )

        def shrink(c, fg, t):
            if t == 0:
                h_slots[c, fg] = work.tile([P, 4, G], BF16, name="h_slots", bufs=2, align_bytes=64)
            j = 4 * fg + t
            b, bank = z_banks[c, fg, t]
            nc.vector.scalar_tensor_tensor(
                out=h_slots[c, fg][:, t, :],
                in0=bank[:],
                scalar=thr[:, j : j + 1],
                in1=aboves[c, fg, t][:],
                op0=ALU.add,
                op1=ALU.min,
            )
            free_banks.append(b)

        def z_slot(c, fg, t):
            for kg in range(KG):
                z_pass(c, fg, t, kg)
            excess(c, fg, t)

        def interleave_h(copy, c, fg, lo, hi):
            if (c, fg) not in h_words:
                h_words[c, fg] = work.tile([P, G, 4], BF16, name="h_words", bufs=2, align_bytes=64)
                h_codes[c, fg] = kept([P, G], U32, "h_codes%d_%d" % (c, fg))
                h_scales[c, fg] = kept([P, G], U8, "h_scales%d_%d" % (c, fg))
            copy(
                out=h_words[c, fg][:, lo:hi, :].rearrange("p (c i) t -> p c t i", i=4),
                in_=h_slots[c, fg][:, :, lo:hi].rearrange("p t (c i) -> p c t i", i=4),
            )

        def quantize_h(c, fg, lo, hi):
            nc.vector.quantize_mx(
                out=h_codes[c, fg][:, lo:hi].bitcast(FP8X4),
                scales=h_scales[c, fg][:, lo:hi],
                in_=h_words[c, fg][:, lo:hi, :].rearrange("p m t -> p (m t)"),
            )

        y_banks, y_rows, y_pairs, y_turned, y_codes = {}, {}, {}, {}, {}
        y_scales = [kept([P, BG, G], U8, "y_scales%d" % c) for c in range(CHUNKS)]

        def y_product(mt, g):
            c, cols = mt // 4, slice((mt % 4) * P, (mt % 4 + 1) * P)
            y_banks[mt, g] = take_bank()
            for fg in range(FG):
                nc.tensor.matmul_mx(
                    out=y_banks[mt, g][1][:],
                    lhsT=h_codes[c, fg][:, cols].bitcast(FP8X4),
                    lhsT_scale=h_scales[c, fg][:, cols],
                    rhs=d_words[fg][:, g * 2 * G : (g + 1) * 2 * G].bitcast(FP4X4),
                    rhs_scale=d_scale[:, fg, g * G : (g + 1) * G],
                    start=(fg == 0),
                    stop=(fg == FG - 1),
                )

        def y_finish(mt, g, round_on=None):
            b, bank = y_banks[mt, g]
            if g == 0:
                y_rows[mt] = work.tile([P, B], F32, name="y_rows", bufs=4)
            bonds = slice(g * G, (g + 1) * G)
            nc.vector.scalar_tensor_tensor(
                out=y_rows[mt][:, bonds], in0=bank[:], scalar=-1.0, in1=hold[:, bonds], op0=ALU.mult, op1=ALU.mult
            )
            free_banks.append(b)
            if True:
                nc.sync.dma_start(out=out_0[mt * P : (mt + 1) * P, bonds], in_=y_rows[mt][:, bonds])
            elif g == BG - 1:
                nc.sync.dma_start(out=out_0[mt * P : (mt + 1) * P, :], in_=y_rows[mt][:])

        def y_round(copy, mt, g):
            y_pairs[mt, g] = work.tile([P, G], BF16, name="y_pairs", bufs=12, align_bytes=64)
            copy(
                out=y_pairs[mt, g][:].rearrange("m (u p e) -> m u p e", u=2, e=2),
                in_=y_rows[mt][:, g * G : (g + 1) * G].rearrange("m (p u e) -> m u p e", u=2, e=2),
            )

        def turn_y(tiles, g, copy=nc.scalar.copy):
            b, bank = take_bank()
            for a, mt in enumerate(tiles):
                words = y_pairs[mt, g][:].bitcast(F32)
                for u in range(2):
                    j = 2 * a + u
                    nc.tensor.transpose(bank[:, j * P : (j + 1) * P], words[:, u * P : (u + 1) * P], ident[:])
            turned = work.tile([P, 2 * G], BF16, name="y_turned", bufs=6, align_bytes=64)
            y_turned[tiles, g] = turned[:, : len(tiles) * G]
            copy_turned(copy, bank, len(tiles), y_turned[tiles, g])
            free_banks.append(b)

        def quantize_y(tiles, g):
            n, first = len(tiles) * P, tiles[0] * P
            if g == 0:
                y_codes[tiles] = kept([P, BG, n], U32, "y_codes%d" % tiles[0])
            c = first // G
            nc.vector.quantize_mx(
                out=y_codes[tiles][:, g, :].bitcast(FP8X4),
                scales=y_scales[c][:, g, first - c * G : first - c * G + n],
                in_=y_turned[tiles, g],
            )

        def store_codes(tiles, lo, hi):
            n, first = len(tiles) * P, tiles[0] * P
            nc.sync.dma_start(
                out=out_1[lo:hi, :, first : first + n, :].rearrange("g p m t -> p g (m t)").bitcast(I32),
                in_=y_codes[tiles][:, lo:hi, :].bitcast(I32),
            )

        def store_scales(first_tile, end_tile, queues):
            c, lo, hi = first_tile // 4, first_tile * P, end_tile * P
            for q in range(4):
                queues[q % len(queues)].dma_start(
                    out=out_2[:, 4 * q : 4 * q + 4, lo:hi].rearrange("g r m -> r g m").bitcast(I32),
                    in_=y_scales[c][32 * q : 32 * q + 4, :, lo - c * G : hi - c * G].bitcast(I32),
                )

        V, S = nc.vector.tensor_copy, nc.scalar.copy
        half = G // 2

        def y_unit(mt, g, copy=S):
            y_product(mt, g)
            y_finish(mt, g)
            y_round(copy, mt, g)

        def y_tile(mt):
            for g in range(BG):
                y_unit(mt, g, V if (g == 2 and mt >= 4) else S)

        def turn_pair(tiles):
            for g in range(BG):
                turn_y(tiles, g)

        def quantize_pair(tiles):
            for g in range(BG):
                quantize_y(tiles, g)
            store_codes(tiles, 0, BG)
            if tiles[-1] == 3:
                store_scales(0, 4, [nc.sync])

        def z_full(c, fg, t):
            z_slot(c, fg, t)
            shrink(c, fg, t)
            if t == 3 and fg == 0:
                interleave_h(V, c, fg, 0, 320)
                interleave_h(S, c, fg, 320, G)
                quantize_h(c, fg, 0, G)
            elif t == 3:
                interleave_h(V, c, fg, 0, half)
                quantize_h(c, fg, 0, half)
                interleave_h(S, c, fg, half, G)
                quantize_h(c, fg, half, G)

        def x_part(c, kg):
            turn_x(c, kg)
            quantize_x(c, kg)

        def head_pass(kg):
            for t in range(4):
                z_pass(0, 0, t, kg)

        def planes(tiles):
            turn_pair(tiles)
            quantize_pair(tiles)

        with tc.manual_schedule():
            turn_x(0, 0)
            b, bank = take_bank()
            for i in range(2):
                nc.tensor.matmul_mx(
                    out=bank[:],
                    lhsT=v_raw[0, 0][:, : 2 * P].bitcast(FP4X4),
                    lhsT_scale=warm_scales[:, :P],
                    rhs=warm_codes[:].bitcast(FP8X4),
                    rhs_scale=warm_scales[:],
                    start=True,
                    stop=True,
                )
            free_banks.append(b)
            sort_v(0, 0)
            quantize_x(0, 0)
            turn_x(0, 1)
            sort_v(1, 0)
            head_pass(0)
            sort_x(0, 2)
            quantize_x(0, 1)
            sort_v(2, 0)
            turn_x(0, 2)
            head_pass(1)
            sort_x(0, 3)
            quantize_x(0, 2)
            sort_v(3, 0)
            turn_x(0, 3)
            sort_x(1, 0)
            head_pass(2)
            quantize_x(0, 3)
            sort_v(0, 1)
            turn_x(1, 0)
            sort_v(1, 1)
            sort_v(2, 1)
            sort_v(3, 1)
            head_pass(3)
            quantize_x(1, 0)
            for t in range(4):
                excess(0, 0, t)
                shrink(0, 0, t)
        interleave_h(V, 0, 0, 0, 320)
        interleave_h(S, 0, 0, 320, G)
        quantize_h(0, 0, 0, G)
        x_part(1, 1)
        z_full(0, 1, 0)
        z_full(0, 1, 1)
        x_part(1, 2)
        x_part(1, 3)
        z_full(0, 1, 2)
        z_full(0, 1, 3)
        z_full(1, 0, 0)
        z_full(1, 0, 1)
        z_full(1, 0, 2)
        z_full(1, 0, 3)
        y_tile(0)
        z_full(1, 1, 0)
        z_full(1, 1, 1)
        y_tile(1)
        z_full(1, 1, 2)
        z_full(1, 1, 3)
        y_tile(2)
        y_tile(3)
        turn_pair((0, 1,))
        quantize_pair((0, 1,))
        y_tile(4)
        y_tile(5)
        turn_pair((2, 3,))
        quantize_pair((2, 3,))
        y_tile(6)
        turn_pair((4, 5,))
        y_unit(7, 0, S)
        y_unit(7, 1, S)
        y_unit(7, 2, V)
        turn_pair((6,))
        quantize_pair((4, 5,))
        quantize_pair((6,))
        for g in range(BG):
            turn_y((7,), g, V if g == 2 else S)
            quantize_y((7,), g)
        store_codes((7,), 0, 3)
        store_scales(4, 8, [nc.sync, nc.scalar])
